import numpy as np
import ml_dtypes


def mxq(x, axis, fmt="e4m3"):
    dtype, down = {"e4m3": (ml_dtypes.float8_e4m3fn, 7), "e5m2": (ml_dtypes.float8_e5m2, 14)}[fmt]
    v = np.moveaxis(np.asarray(x, np.float32).astype(ml_dtypes.bfloat16).astype(np.float64), axis, -1)
    blocks = v.reshape(v.shape[:-1] + (-1, 32))
    amax = np.abs(blocks).max(-1, keepdims=True)
    byte = np.maximum(np.where(amax > 0, np.frexp(amax)[1] - 1 + 127, 0) - down, 1)
    scale = np.exp2(byte - 127.0)
    codes = (blocks / scale).astype(np.float32).astype(dtype).astype(np.float64)
    return np.moveaxis((codes * scale).reshape(v.shape), -1, axis)


WIDE = False


def mx_kscale(k):
    if not WIDE:
        return np.ones(k)
    levels = np.array([10, -10, 5, -5, 0])
    if k % 512:
        return np.exp2(np.random.permutation(np.resize(levels, k // 32))).repeat(32)
    a = np.empty((k // 512, 16))
    for p in range(k // 512):
        a[p, :8] = np.random.permutation(np.resize(levels, 8))
        for g in range(8):
            far = levels[np.abs(levels - a[p, g]) >= 10]
            a[p, g + 8] = far[np.random.randint(len(far))]
    return np.exp2(a.ravel()).repeat(32)


def f64(x):
    return np.asarray(x).astype(np.float64)


def striped(idx):
    return np.tile(idx.reshape(-1, 16).T, (8, 1)).astype(np.uint16)


def unstriped(offs):
    return offs[:16].T.reshape(-1).astype(np.int64)


def pack_weight(w):
    k, n = w.shape
    w = f64(np.asarray(w, np.float32).astype(ml_dtypes.bfloat16)).reshape(k // 32, 32, n)
    amax = np.abs(w).max(1)
    byte = np.clip(np.where(amax > 0, np.frexp(amax)[1] - 1 + 127 - 7, 1), 1, 254)
    scaled = (w * np.exp2(127.0 - byte)[:, None, :]).reshape(k, n).astype(np.float32)
    words = np.ascontiguousarray(scaled.reshape(k // 512, 128, 4, n).transpose(0, 1, 3, 2)).astype(ml_dtypes.float8_e4m3fn).view(np.uint8)
    return words, np.ascontiguousarray(byte.astype(np.uint8).reshape(k // 512, 16, n))


def unpack_weight(words, scales):
    g, p, n, _ = words.shape
    vals = np.ascontiguousarray(words).view(ml_dtypes.float8_e4m3fn).astype(np.float64) * np.repeat(np.exp2(scales.astype(np.float64) - 127.0), 8, axis=1)[..., None]
    return vals.transpose(0, 1, 3, 2).reshape(g * 512, n)


def sigmoid(v):
    return 1.0 / (1.0 + np.exp(-np.maximum(v, -700.0)))


K, T, S, D, H, Z, W = 512, 2048, 512, 2, 512, 512, 2048
P = 2 ** 7


def setup_inputs():
    n = np.random.standard_normal
    s = mx_kscale(K)[:, None]
    packed_xT = pack_weight(n((K, T)) * s)
    packed_eT = pack_weight(n((K, W)) * s)
    return {
        "x_words": packed_xT[0],
        "x_scales": packed_xT[1],
        "w1": (n((K, H)) / np.sqrt(K) / s).astype(np.float32),
        "w2": (n((K, H)) / np.sqrt(K) / s).astype(np.float32),
        "e_words": packed_eT[0],
        "e_scales": packed_eT[1],
        "unit": (np.random.uniform(0.6, 1.4, (K, 1)) / np.sqrt(K) / s).astype(np.float32),
        "ndw": (np.tile(np.random.uniform(0.2, 1.2, W), (P, 1))).astype(np.float32),
        "offs": striped(np.random.permutation(T)[:S]),
        "qry": striped(np.random.permutation(W)[:Z]),
        "prtn": striped(np.random.permutation(Z)),
    }


def reference(x_words, x_scales, w1, w2, e_words, e_scales, unit, ndw, offs, qry, prtn):
    xq = unpack_weight(x_words, x_scales)[:, unstriped(offs)]
    y = mxq(f64(w1), 0, "e4m3").T @ xq
    yg = mxq(f64(w2), 0, "e4m3").T @ xq
    yw = y * sigmoid(yg)
    pass_ = yw.reshape(len(yw), -1, D).max(axis=2)
    p2 = (pass_) ** 2
    ms = p2.mean(axis=1, keepdims=True)
    np_ = pass_ / np.sqrt(ms + 0.1)
    hid = f64(unit) * np_
    e_qry = unpack_weight(e_words, e_scales)[:, unstriped(qry)]
    sc = mxq(hid, 0, "e4m3").T @ e_qry
    spar = sc[:, unstriped(prtn)]
    gap = sc - spar
    return (np.log(np.exp(-1.5 * np.tanh(gap)) + 0.5)) * (f64(ndw)[:1][:, unstriped(qry)])

@@ -1,0 +1,212 @@
+import math
+from contextlib import ExitStack
+
+import concourse.mybir as mybir
+
+K, T, S, H, Z, W = 512, 2048, 512, 512, 512, 2048
+V = S // 2
+P = 128
+PACK = 4
+FLOPS = 2 * K * H * S * 2 + 2 * H * V * Z
+
+F32 = mybir.dt.float32
+BF16 = mybir.dt.bfloat16
+U32 = mybir.dt.uint32
+I32 = mybir.dt.int32
+U16 = mybir.dt.uint16
+U8 = mybir.dt.uint8
+FP8X4 = mybir.dt.float8_e4m3fn_x4
+ALU = mybir.AluOpType
+ACT = mybir.ActivationFunctionType
+
+EPS = 0.1
+POOL_PITCH = V + 8
+HALF = Z // 2
+OUT_COLS = 128
+
+
+def tile_picked_yrerank_pair_p_kernel(
+    tc, x_words, x_scales, w1, w2, e_words, e_scales, unit, ndw, offs, qry, prtn, out
+):
+    nc = tc.nc
+    with ExitStack() as ctx:
+        sb = ctx.enter_context(tc.tile_pool(name="sb", bufs=1))
+        ps = ctx.enter_context(tc.psum_pool(name="ps", bufs=1))
+
+        def tile(name, shape, dtype, tag=None):
+            return sb.tile(shape, dtype, name=name, tag=tag or name, align_bytes=64)
+
+        def load_words(name, words):
+            table = tile(name, [P, words.shape[2]], U32)
+            nc.sync.dma_start(table[:].bitcast(I32), words[0].rearrange("p n t -> p (n t)").bitcast(I32))
+            return table
+
+        def load_scales(name, scales):
+            table = tile(name, [P, scales.shape[2]], U8)
+            for q in range(4):
+                rows = scales[0, 4 * q : 4 * q + 4, :].bitcast(I32)
+                nc.sync.dma_start(
+                    table[32 * q : 32 * q + 32, :].bitcast(I32), rows.unsqueeze(0).to_broadcast([8] + list(rows.shape))
+                )
+            return table
+
+        def load_list(name, entries):
+            offsets = tile(name, [P, entries.shape[1]], U16)
+            nc.sync.dma_start(offsets[:], entries)
+            return offsets
+
+        def load_weight(name, w):
+            raw = tile(name, [P, PACK, H], F32)
+            nc.sync.dma_start(raw[:], w.rearrange("(p j) c -> p j c", j=PACK))
+            return raw
+
+        def gather(name, table, offsets, dtype, tag=None):
+            picked = tile(name, [P, 16 * offsets.shape[1]], dtype, tag)
+            nc.vector.tensor_copy(picked[:], table[:].indirect(offsets[:]))
+            return picked
+
+        def round_weight(name, raw):
+            pairs = []
+            source = raw[:].rearrange("p j (m u t) -> p u m j t", u=2, t=2)
+            for u, copy in enumerate((nc.vector.tensor_copy, nc.scalar.copy)):
+                pair = tile("%s_bf%d" % (name, u), [P, 2, P, PACK], BF16)
+                copy(pair[:].rearrange("p t m j -> p m j t"), source[:, u])
+                pairs.append(pair)
+            return [pairs[t // 2][:, t % 2].rearrange("p m j -> p (m j)") for t in range(PACK)]
+
+        def quantize(name, values):
+            width = values.shape[1] // PACK
+            codes = tile(name + "_codes", [P, width], U32)
+            scales = tile(name + "_scales", [P, width], U8)
+            nc.vector.quantize_mx(out=codes[:].bitcast(FP8X4), scales=scales[:], in_=values)
+            return codes, scales
+
+        def product(bank, stationary, moving):
+            nc.tensor.matmul_mx(
+                out=bank[:],
+                lhsT=stationary[0][:].bitcast(FP8X4),
+                lhsT_scale=stationary[1][:],
+                rhs=moving[0][:].bitcast(FP8X4),
+                rhs_scale=moving[1][:],
+                start=True,
+                stop=True,
+            )
+
+        offs_sb = load_list("offs_sb", offs)
+        qry_sb = load_list("qry_sb", qry)
+        w2_raw = load_weight("w2_raw", w2)
+        xs_table = load_scales("xs_table", x_scales)
+        xw_table = load_words("xw_table", x_words)
+        es_table = load_scales("es_table", e_scales)
+        w1_raw = load_weight("w1_raw", w1)
+        unit_sb = tile("unit_sb", [P, PACK], F32)
+        nc.sync.dma_start(unit_sb[:], unit.rearrange("(p t) o -> p (t o)", t=PACK))
+        prtn_sb = load_list("prtn_sb", prtn)
+        ew_table = load_words("ew_table", e_words)
+        ndw_table = tile("ndw_table", [P, W], F32)
+        nc.sync.dma_start(ndw_table[:], ndw)
+
+        pooled = tile("pooled", [P, PACK, POOL_PITCH], F32)
+        ones = tile("ones", [P, PACK], F32)
+        nc.gpsimd.memset(ones[:], 1.0)
+        nc.gpsimd.tensor_scalar(pooled[:, :, V], ones[:], math.sqrt(4.0 * EPS * V), 0.0, ALU.mult, ALU.add)
+        minus_half = tile("minus_half", [P, 1], F32)
+        nc.gpsimd.memset(minus_half[:], -0.5)
+
+        x_bytes = gather("x_bytes", xs_table, offs_sb, U8)
+        w2_bf = round_weight("w2", w2_raw)
+        w2_q = [quantize("w2_%d" % t, w2_bf[t]) for t in range(PACK)]
+        x_picked = (gather("x_codes", xw_table, offs_sb, U32), x_bytes)
+        gates = []
+        for t in range(PACK):
+            bank = ps.tile([P, S], F32, name="gate_bank%d" % t, tag="bank%d" % t)
+            product(bank, w2_q[t], x_picked)
+            gates.append(bank)
+        e_bytes = gather("e_bytes", es_table, qry_sb, U8)
+
+        def gate(t):
+            th = tile("th%d" % t, [P, 2, V], F32)
+            nc.scalar.activation(th[:], gates[t][:].rearrange("p (v d) -> p d v", d=2), ACT.Tanh, scale=0.5)
+            return th
+
+        ths = [gate(0)]
+        w1_bf = round_weight("w1", w1_raw)
+        values = []
+        for t in range(PACK):
+            bank = ps.tile([P, S], F32, name="value_bank%d" % t, tag="bank%d" % (PACK + t))
+            product(bank, quantize("w1_%d" % t, w1_bf[t]), x_picked)
+            values.append(bank)
+        for t in range(1, PACK):
+            ths.append(gate(t))
+
+        hid_planes = tile("hid_planes", [P, PACK, V], BF16)
+        for t in range(PACK):
+            gated = tile("gated%d" % t, [P, 2, V], F32)
+            nc.vector.scalar_tensor_tensor(
+                gated[:], ths[t][:], 1.0, values[t][:].rearrange("p (v d) -> p d v", d=2), ALU.add, ALU.mult
+            )
+            nc.vector.tensor_tensor(pooled[:, t, :V], gated[:, 0, :], gated[:, 1, :], ALU.max)
+            squares = tile("squares%d" % t, [P, V + 1], BF16)
+            mean_sq = tile("mean_sq%d" % t, [P, 1], F32)
+            nc.scalar.activation(squares[:], pooled[:, t, : V + 1], ACT.Square, scale=1.0 / math.sqrt(V), accum_out=mean_sq[:])
+            inv_rms = tile("inv_rms%d" % t, [P, 1], F32)
+            nc.gpsimd.tensor_tensor(inv_rms[:], mean_sq[:], minus_half[:], ALU.pow)
+            if t < PACK - 1:
+                factor = tile("factor%d" % t, [P, 1], F32)
+                nc.gpsimd.tensor_tensor(factor[:], inv_rms[:], unit_sb[:, t : t + 1], ALU.mult)
+                nc.scalar.activation(hid_planes[:, t, :], pooled[:, t, :V], ACT.Copy, scale=factor[:])
+            else:
+                e_picked = (gather("e_codes", ew_table, qry_sb, U32, "gated%d" % t), e_bytes)
+                nc.vector.tensor_scalar(
+                    hid_planes[:, t, :], pooled[:, t, :V], inv_rms[:], unit_sb[:, t : t + 1], ALU.mult, ALU.mult
+                )
+
+        weight = tile("weight", [P, Z], F32, "squares%d" % (PACK - 1))
+        nc.scalar.activation(weight[:], ndw_table[:].indirect(qry_sb[:]), ACT.Copy)
+
+        hids = []
+        for h in range(2):
+            hid = tile("hid%d" % h, [P, P, PACK], BF16)
+            nc.vector.tensor_copy(
+                hid[:].rearrange("p (c i) t -> p c t i", i=4),
+                hid_planes[:, :, h * P : (h + 1) * P].rearrange("p t (c i) -> p c t i", i=4),
+            )
+            hids.append(hid)
+        banks, scores = [], []
+        for h in range(2):
+            bank = ps.tile([P, Z], F32, name="score_bank%d" % h, tag="bank%d" % h)
+            product(bank, quantize("hid%d" % h, hids[h][:].rearrange("p v t -> p (v t)")), e_picked)
+            score = tile("score%d" % h, [P, Z], F32)
+            nc.scalar.copy(score[:], bank[:])
+            banks.append(bank)
+            scores.append(score)
+
+        gap = tile("gap", [P, 2, Z], F32)
+        squashed = tile("squashed", [P, 2, Z], F32)
+        grown = tile("grown", [P, 2, Z], F32)
+        for h in range(2):
+            partners = []
+            for c in range(2):
+                partner = tile("partner%d_%d" % (h, c), [P, HALF], F32)
+                window = scores[h][:].indirect(prtn_sb[:, c * HALF // 16 : (c + 1) * HALF // 16])
+                if (h, c) == (0, 1):
+                    nc.scalar.activation(partner[:], window, ACT.Copy)
+                else:
+                    nc.vector.tensor_copy(partner[:], window)
+                partners.append(partner)
+            for c in range(2):
+                cols = slice(c * HALF, (c + 1) * HALF)
+                nc.vector.tensor_tensor(gap[:, h, cols], banks[h][:, cols], partners[c][:], ALU.subtract)
+                nc.scalar.activation(squashed[:, h, cols], gap[:, h, cols], ACT.Tanh)
+            nc.scalar.activation(grown[:, h, :], squashed[:, h, :], ACT.Exp, scale=-1.5)
+
+        out_view = out.rearrange("(h p) e -> p h e", h=2)
+        for c in range(Z // OUT_COLS):
+            cols = slice(c * OUT_COLS, (c + 1) * OUT_COLS)
+            logs = tile("logs%d" % c, [P, 2, OUT_COLS], F32)
+            nc.scalar.activation(logs[:], grown[:, :, cols], ACT.Ln, bias=0.5)
+            result = tile("result%d" % c, [P, 2, OUT_COLS], F32)
+            nc.vector.tensor_tensor(
+                result[:], logs[:], weight[:, cols].unsqueeze(1).to_broadcast([P, 2, OUT_COLS]), ALU.mult
+            )
+            nc.sync.dma_start(out_view[:, :, cols], result[:])

@@ -36,18 +36,16 @@ def tile_picked_yrerank_pair_p_kernel(
         def tile(name, shape, dtype, tag=None):
             return sb.tile(shape, dtype, name=name, tag=tag or name, align_bytes=64)
 
-        def load_words(name, words):
-            table = tile(name, [P, words.shape[2]], U32)
+        def load_words(name, words, tag=None):
+            table = tile(name, [P, words.shape[2]], U32, tag)
             nc.sync.dma_start(table[:].bitcast(I32), words[0].rearrange("p n t -> p (n t)").bitcast(I32))
             return table
 
-        def load_scales(name, scales):
+        def load_scales(name, scales, clear, queue):
             table = tile(name, [P, scales.shape[2]], U8)
-            for q in range(4):
-                rows = scales[0, 4 * q : 4 * q + 4, :].bitcast(I32)
-                nc.sync.dma_start(
-                    table[32 * q : 32 * q + 32, :].bitcast(I32), rows.unsqueeze(0).to_broadcast([8] + list(rows.shape))
-                )
+            clear.memset(table[:].bitcast(I32), 0)
+            for r in range(4):
+                queue.dma_start(table[r:P:32, :].bitcast(I32), scales[0, r:16:4, :].bitcast(I32))
             return table
 
         def load_list(name, entries):
@@ -65,14 +63,12 @@ def tile_picked_yrerank_pair_p_kernel(
             nc.vector.tensor_copy(picked[:], table[:].indirect(offsets[:]))
             return picked
 
-        def round_weight(name, raw):
-            pairs = []
+        def round_weight(name, raw, copies, tag=None):
+            rounded = tile(name, [P, 2, 2, P, PACK], BF16, tag)
             source = raw[:].rearrange("p j (m u t) -> p u m j t", u=2, t=2)
-            for u, copy in enumerate((nc.vector.tensor_copy, nc.scalar.copy)):
-                pair = tile("%s_bf%d" % (name, u), [P, 2, P, PACK], BF16)
-                copy(pair[:].rearrange("p t m j -> p m j t"), source[:, u])
-                pairs.append(pair)
-            return [pairs[t // 2][:, t % 2].rearrange("p m j -> p (m j)") for t in range(PACK)]
+            for u in range(2):
+                copies[u](rounded[:, u].rearrange("p t m j -> p m j t"), source[:, u])
+            return [rounded[:, t // 2, t % 2].rearrange("p m j -> p (m j)") for t in range(PACK)]
 
         def quantize(name, values):
             width = values.shape[1] // PACK
@@ -95,16 +91,11 @@ def tile_picked_yrerank_pair_p_kernel(
         offs_sb = load_list("offs_sb", offs)
         qry_sb = load_list("qry_sb", qry)
         w2_raw = load_weight("w2_raw", w2)
-        xs_table = load_scales("xs_table", x_scales)
         xw_table = load_words("xw_table", x_words)
-        es_table = load_scales("es_table", e_scales)
         w1_raw = load_weight("w1_raw", w1)
-        unit_sb = tile("unit_sb", [P, PACK], F32)
-        nc.sync.dma_start(unit_sb[:], unit.rearrange("(p t) o -> p (t o)", t=PACK))
         prtn_sb = load_list("prtn_sb", prtn)
-        ew_table = load_words("ew_table", e_words)
-        ndw_table = tile("ndw_table", [P, W], F32)
-        nc.sync.dma_start(ndw_table[:], ndw)
+        xs_table = load_scales("xs_table", x_scales, nc.vector, nc.scalar)
+        es_table = load_scales("es_table", e_scales, nc.gpsimd, nc.gpsimd)
 
         pooled = tile("pooled", [P, PACK, POOL_PITCH], F32)
         ones = tile("ones", [P, PACK], F32)
@@ -113,33 +104,36 @@ def tile_picked_yrerank_pair_p_kernel(
         minus_half = tile("minus_half", [P, 1], F32)
         nc.gpsimd.memset(minus_half[:], -0.5)
 
-        x_bytes = gather("x_bytes", xs_table, offs_sb, U8)
-        w2_bf = round_weight("w2", w2_raw)
+        w2_bf = round_weight("w2_bf", w2_raw, (nc.vector.tensor_copy, nc.scalar.copy))
+        ew_table = load_words("ew_table", e_words, "w2_raw")
         w2_q = [quantize("w2_%d" % t, w2_bf[t]) for t in range(PACK)]
-        x_picked = (gather("x_codes", xw_table, offs_sb, U32), x_bytes)
+        unit_sb = tile("unit_sb", [P, PACK], F32, "w2_bf")
+        nc.sync.dma_start(unit_sb[:], unit.rearrange("(p t) o -> p (t o)", t=PACK))
+        x_bytes = gather("x_bytes", xs_table, offs_sb, U8)
+        x_picked = (gather("x_codes", xw_table, offs_sb, U32, "xs_table"), x_bytes)
         gates = []
         for t in range(PACK):
             bank = ps.tile([P, S], F32, name="gate_bank%d" % t, tag="bank%d" % t)
             product(bank, w2_q[t], x_picked)
             gates.append(bank)
-        e_bytes = gather("e_bytes", es_table, qry_sb, U8)
+        e_bytes = gather("e_bytes", es_table, qry_sb, U8, "xw_table")
 
         def gate(t):
             th = tile("th%d" % t, [P, 2, V], F32)
             nc.scalar.activation(th[:], gates[t][:].rearrange("p (v d) -> p d v", d=2), ACT.Tanh, scale=0.5)
             return th
 
-        ths = [gate(0)]
-        w1_bf = round_weight("w1", w1_raw)
+        ths = [gate(t) for t in range(PACK)]
+        w1_bf = round_weight("w1_bf", w1_raw, (nc.vector.tensor_copy, nc.vector.tensor_copy), "es_table")
+        ndw_table = tile("ndw_table", [P, W], F32, "w1_raw")
+        nc.sync.dma_start(ndw_table[:], ndw)
         values = []
         for t in range(PACK):
             bank = ps.tile([P, S], F32, name="value_bank%d" % t, tag="bank%d" % (PACK + t))
             product(bank, quantize("w1_%d" % t, w1_bf[t]), x_picked)
             values.append(bank)
-        for t in range(1, PACK):
-            ths.append(gate(t))
 
-        hid_planes = tile("hid_planes", [P, PACK, V], BF16)
+        inv_rms = []
         for t in range(PACK):
             gated = tile("gated%d" % t, [P, 2, V], F32)
             nc.vector.scalar_tensor_tensor(
@@ -149,17 +143,15 @@ def tile_picked_yrerank_pair_p_kernel(
             squares = tile("squares%d" % t, [P, V + 1], BF16)
             mean_sq = tile("mean_sq%d" % t, [P, 1], F32)
             nc.scalar.activation(squares[:], pooled[:, t, : V + 1], ACT.Square, scale=1.0 / math.sqrt(V), accum_out=mean_sq[:])
-            inv_rms = tile("inv_rms%d" % t, [P, 1], F32)
-            nc.gpsimd.tensor_tensor(inv_rms[:], mean_sq[:], minus_half[:], ALU.pow)
-            if t < PACK - 1:
-                factor = tile("factor%d" % t, [P, 1], F32)
-                nc.gpsimd.tensor_tensor(factor[:], inv_rms[:], unit_sb[:, t : t + 1], ALU.mult)
-                nc.scalar.activation(hid_planes[:, t, :], pooled[:, t, :V], ACT.Copy, scale=factor[:])
-            else:
-                e_picked = (gather("e_codes", ew_table, qry_sb, U32, "gated%d" % t), e_bytes)
-                nc.vector.tensor_scalar(
-                    hid_planes[:, t, :], pooled[:, t, :V], inv_rms[:], unit_sb[:, t : t + 1], ALU.mult, ALU.mult
-                )
+            inv_rms.append(tile("inv_rms%d" % t, [P, 1], F32))
+            nc.gpsimd.tensor_tensor(inv_rms[t][:], mean_sq[:], minus_half[:], ALU.pow)
+
+        e_picked = (gather("e_codes", ew_table, qry_sb, U32, "gated%d" % (PACK - 1)), e_bytes)
+        hid_planes = tile("hid_planes", [P, PACK, V], BF16, "gated%d" % (PACK - 2))
+        for t in range(PACK):
+            nc.vector.tensor_scalar(
+                hid_planes[:, t, :], pooled[:, t, :V], inv_rms[t][:], unit_sb[:, t : t + 1], ALU.mult, ALU.mult
+            )
 
         weight = tile("weight", [P, Z], F32, "squares%d" % (PACK - 1))
         nc.scalar.activation(weight[:], ndw_table[:].indirect(qry_sb[:]), ACT.Copy)
@@ -184,20 +176,22 @@ def tile_picked_yrerank_pair_p_kernel(
         gap = tile("gap", [P, 2, Z], F32)
         squashed = tile("squashed", [P, 2, Z], F32)
         grown = tile("grown", [P, 2, Z], F32)
+        partners = {}
         for h in range(2):
-            partners = []
             for c in range(2):
                 partner = tile("partner%d_%d" % (h, c), [P, HALF], F32)
                 window = scores[h][:].indirect(prtn_sb[:, c * HALF // 16 : (c + 1) * HALF // 16])
-                if (h, c) == (0, 1):
-                    nc.scalar.activation(partner[:], window, ACT.Copy)
-                else:
+                if h == 0:
                     nc.vector.tensor_copy(partner[:], window)
-                partners.append(partner)
+                else:
+                    nc.scalar.activation(partner[:], window, ACT.Copy)
+                partners[h, c] = partner
+        for h in range(2):
             for c in range(2):
                 cols = slice(c * HALF, (c + 1) * HALF)
-                nc.vector.tensor_tensor(gap[:, h, cols], banks[h][:, cols], partners[c][:], ALU.subtract)
+                nc.vector.tensor_tensor(gap[:, h, cols], banks[h][:, cols], partners[h, c][:], ALU.subtract)
                 nc.scalar.activation(squashed[:, h, cols], gap[:, h, cols], ACT.Tanh)
+        for h in range(2):
             nc.scalar.activation(grown[:, h, :], squashed[:, h, :], ACT.Exp, scale=-1.5)
 
         out_view = out.rearrange("(h p) e -> p h e", h=2)

@@ -20,6 +20,7 @@ ALU = mybir.AluOpType
 ACT = mybir.ActivationFunctionType
 
 EPS = 0.1
+W2_VECTOR_COLS = 88
 POOL_PITCH = V + 8
 HALF = Z // 2
 OUT_COLS = 128
@@ -61,29 +62,22 @@ def tile_picked_yrerank_pair_p_kernel(
         def gather(name, table, offsets, dtype, tag=None):
             picked = tile(name, [P, 16 * offsets.shape[1]], dtype, tag)
             nc.vector.tensor_copy(picked[:], table[:].indirect(offsets[:]))
-            return picked
-
-        def round_weight(name, raw, copies, tag=None):
-            rounded = tile(name, [P, 2, 2, P, PACK], BF16, tag)
-            source = raw[:].rearrange("p j (m u t) -> p u m j t", u=2, t=2)
-            for u in range(2):
-                copies[u](rounded[:, u].rearrange("p t m j -> p m j t"), source[:, u])
-            return [rounded[:, t // 2, t % 2].rearrange("p m j -> p (m j)") for t in range(PACK)]
+            return picked[:]
 
         def quantize(name, values):
             width = values.shape[1] // PACK
             codes = tile(name + "_codes", [P, width], U32)
             scales = tile(name + "_scales", [P, width], U8)
             nc.vector.quantize_mx(out=codes[:].bitcast(FP8X4), scales=scales[:], in_=values)
-            return codes, scales
+            return codes[:], scales[:]
 
         def product(bank, stationary, moving):
             nc.tensor.matmul_mx(
                 out=bank[:],
-                lhsT=stationary[0][:].bitcast(FP8X4),
-                lhsT_scale=stationary[1][:],
-                rhs=moving[0][:].bitcast(FP8X4),
-                rhs_scale=moving[1][:],
+                lhsT=stationary[0].bitcast(FP8X4),
+                lhsT_scale=stationary[1],
+                rhs=moving[0].bitcast(FP8X4),
+                rhs_scale=moving[1],
                 start=True,
                 stop=True,
             )
@@ -104,9 +98,13 @@ def tile_picked_yrerank_pair_p_kernel(
         minus_half = tile("minus_half", [P, 1], F32)
         nc.gpsimd.memset(minus_half[:], -0.5)
 
-        w2_bf = round_weight("w2_bf", w2_raw, (nc.vector.tensor_copy, nc.scalar.copy))
+        w2_bf = tile("w2_bf", [P, PACK, P, PACK], BF16)
+        w2_dealt = w2_bf[:].rearrange("p t m j -> p m j t")
+        w2_source = w2_raw[:].rearrange("p j (m t) -> p m j t", t=PACK)
+        nc.vector.tensor_copy(w2_dealt[:, :W2_VECTOR_COLS], w2_source[:, :W2_VECTOR_COLS])
+        nc.scalar.copy(w2_dealt[:, W2_VECTOR_COLS:], w2_source[:, W2_VECTOR_COLS:])
         ew_table = load_words("ew_table", e_words, "w2_raw")
-        w2_q = [quantize("w2_%d" % t, w2_bf[t]) for t in range(PACK)]
+        w2_codes, w2_scales = quantize("w2", w2_bf[:].rearrange("p t m j -> p (t m j)"))
         unit_sb = tile("unit_sb", [P, PACK], F32, "w2_bf")
         nc.sync.dma_start(unit_sb[:], unit.rearrange("(p t) o -> p (t o)", t=PACK))
         x_bytes = gather("x_bytes", xs_table, offs_sb, U8)
@@ -114,9 +112,8 @@ def tile_picked_yrerank_pair_p_kernel(
         gates = []
         for t in range(PACK):
             bank = ps.tile([P, S], F32, name="gate_bank%d" % t, tag="bank%d" % t)
-            product(bank, w2_q[t], x_picked)
+            product(bank, (w2_codes[:, t * P : (t + 1) * P], w2_scales[:, t * P : (t + 1) * P]), x_picked)
             gates.append(bank)
-        e_bytes = gather("e_bytes", es_table, qry_sb, U8, "xw_table")
 
         def gate(t):
             th = tile("th%d" % t, [P, 2, V], F32)
@@ -124,16 +121,21 @@ def tile_picked_yrerank_pair_p_kernel(
             return th
 
         ths = [gate(t) for t in range(PACK)]
-        w1_bf = round_weight("w1_bf", w1_raw, (nc.vector.tensor_copy, nc.vector.tensor_copy), "es_table")
+        w1_bf = tile("w1_bf", [P, PACK, P, PACK], BF16, "xw_table")
+        w1_source = w1_raw[:].rearrange("p j (m t) -> p m j t", t=PACK)
+        for t in range(0, PACK, 2):
+            nc.vector.tensor_copy(w1_bf[:, t : t + 2].rearrange("p t m j -> p m j t"), w1_source[:, :, :, t : t + 2])
         ndw_table = tile("ndw_table", [P, W], F32, "w1_raw")
         nc.sync.dma_start(ndw_table[:], ndw)
         values = []
         for t in range(PACK):
             bank = ps.tile([P, S], F32, name="value_bank%d" % t, tag="bank%d" % (PACK + t))
-            product(bank, quantize("w1_%d" % t, w1_bf[t]), x_picked)
+            product(bank, quantize("w1_%d" % t, w1_bf[:, t].rearrange("p m j -> p (m j)")), x_picked)
             values.append(bank)
 
-        inv_rms = []
+        e_bytes = gather("e_bytes", es_table, qry_sb, U8, "xw_table")
+        hid_planes = tile("hid_planes", [P, PACK, V], BF16)
+        last = PACK - 1
         for t in range(PACK):
             gated = tile("gated%d" % t, [P, 2, V], F32)
             nc.vector.scalar_tensor_tensor(
@@ -143,18 +145,17 @@ def tile_picked_yrerank_pair_p_kernel(
             squares = tile("squares%d" % t, [P, V + 1], BF16)
             mean_sq = tile("mean_sq%d" % t, [P, 1], F32)
             nc.scalar.activation(squares[:], pooled[:, t, : V + 1], ACT.Square, scale=1.0 / math.sqrt(V), accum_out=mean_sq[:])
-            inv_rms.append(tile("inv_rms%d" % t, [P, 1], F32))
-            nc.gpsimd.tensor_tensor(inv_rms[t][:], mean_sq[:], minus_half[:], ALU.pow)
-
-        e_picked = (gather("e_codes", ew_table, qry_sb, U32, "gated%d" % (PACK - 1)), e_bytes)
-        hid_planes = tile("hid_planes", [P, PACK, V], BF16, "gated%d" % (PACK - 2))
-        for t in range(PACK):
-            nc.vector.tensor_scalar(
-                hid_planes[:, t, :], pooled[:, t, :V], inv_rms[t][:], unit_sb[:, t : t + 1], ALU.mult, ALU.mult
-            )
-
-        weight = tile("weight", [P, Z], F32, "squares%d" % (PACK - 1))
-        nc.scalar.activation(weight[:], ndw_table[:].indirect(qry_sb[:]), ACT.Copy)
+            inv_rms = tile("inv_rms%d" % t, [P, 1], F32)
+            nc.gpsimd.tensor_tensor(inv_rms[:], mean_sq[:], minus_half[:], ALU.pow)
+            if t < last:
+                factor = tile("factor%d" % t, [P, 1], F32)
+                nc.gpsimd.tensor_tensor(factor[:], inv_rms[:], unit_sb[:, t : t + 1], ALU.mult)
+                nc.scalar.activation(hid_planes[:, t, :], pooled[:, t, :V], ACT.Copy, scale=factor[:])
+            else:
+                e_picked = (gather("e_codes", ew_table, qry_sb, U32, "gated%d" % last), e_bytes)
+                nc.vector.tensor_scalar(
+                    hid_planes[:, t, :], pooled[:, t, :V], inv_rms[:], unit_sb[:, t : t + 1], ALU.mult, ALU.mult
+                )
 
         hids = []
         for h in range(2):
@@ -172,6 +173,8 @@ def tile_picked_yrerank_pair_p_kernel(
             nc.scalar.copy(score[:], bank[:])
             banks.append(bank)
             scores.append(score)
+
+        weight = gather("weight", ndw_table, qry_sb, F32, "hid1")
 
         gap = tile("gap", [P, 2, Z], F32)
         squashed = tile("squashed", [P, 2, Z], F32)

@@ -20,10 +20,10 @@ ALU = mybir.AluOpType
 ACT = mybir.ActivationFunctionType
 
 EPS = 0.1
-W2_VECTOR_COLS = 88
+VECTOR_COLS = 88
 POOL_PITCH = V + 8
+SCALAR_PLANES = 2
 HALF = Z // 2
-OUT_COLS = 128
 
 
 def tile_picked_yrerank_pair_p_kernel(
@@ -42,11 +42,13 @@ def tile_picked_yrerank_pair_p_kernel(
             nc.sync.dma_start(table[:].bitcast(I32), words[0].rearrange("p n t -> p (n t)").bitcast(I32))
             return table
 
-        def load_scales(name, scales, clear, queue):
+        def load_scales(name, scales):
             table = tile(name, [P, scales.shape[2]], U8)
-            clear.memset(table[:].bitcast(I32), 0)
-            for r in range(4):
-                queue.dma_start(table[r:P:32, :].bitcast(I32), scales[0, r:16:4, :].bitcast(I32))
+            for q in range(4):
+                rows = scales[0, 4 * q : 4 * q + 4, :].bitcast(I32)
+                nc.sync.dma_start(
+                    table[32 * q : 32 * q + 32, :].bitcast(I32), rows.unsqueeze(0).to_broadcast([8] + list(rows.shape))
+                )
             return table
 
         def load_list(name, entries):
@@ -85,11 +87,16 @@ def tile_picked_yrerank_pair_p_kernel(
         offs_sb = load_list("offs_sb", offs)
         qry_sb = load_list("qry_sb", qry)
         w2_raw = load_weight("w2_raw", w2)
+        xs_table = load_scales("xs_table", x_scales)
         xw_table = load_words("xw_table", x_words)
+        es_table = load_scales("es_table", e_scales)
         w1_raw = load_weight("w1_raw", w1)
+        unit_sb = tile("unit_sb", [P, PACK], F32)
+        nc.sync.dma_start(unit_sb[:], unit.rearrange("(p t) o -> p (t o)", t=PACK))
         prtn_sb = load_list("prtn_sb", prtn)
-        xs_table = load_scales("xs_table", x_scales, nc.vector, nc.scalar)
-        es_table = load_scales("es_table", e_scales, nc.gpsimd, nc.gpsimd)
+        ew_table = load_words("ew_table", e_words)
+        ndw_table = tile("ndw_table", [P, W], F32)
+        nc.sync.dma_start(ndw_table[:], ndw)
 
         pooled = tile("pooled", [P, PACK, POOL_PITCH], F32)
         ones = tile("ones", [P, PACK], F32)
@@ -98,64 +105,75 @@ def tile_picked_yrerank_pair_p_kernel(
         minus_half = tile("minus_half", [P, 1], F32)
         nc.gpsimd.memset(minus_half[:], -0.5)
 
-        w2_bf = tile("w2_bf", [P, PACK, P, PACK], BF16)
-        w2_dealt = w2_bf[:].rearrange("p t m j -> p m j t")
-        w2_source = w2_raw[:].rearrange("p j (m t) -> p m j t", t=PACK)
-        nc.vector.tensor_copy(w2_dealt[:, :W2_VECTOR_COLS], w2_source[:, :W2_VECTOR_COLS])
-        nc.scalar.copy(w2_dealt[:, W2_VECTOR_COLS:], w2_source[:, W2_VECTOR_COLS:])
-        ew_table = load_words("ew_table", e_words, "w2_raw")
+        def round_weight(name, raw):
+            rounded = tile(name, [P, PACK, P, PACK], BF16)
+            dealt = rounded[:].rearrange("p t m j -> p m j t")
+            source = raw[:].rearrange("p j (m t) -> p m j t", t=PACK)
+            nc.vector.tensor_copy(dealt[:, :VECTOR_COLS], source[:, :VECTOR_COLS])
+            nc.scalar.copy(dealt[:, VECTOR_COLS:], source[:, VECTOR_COLS:])
+            return rounded
+
+        w2_bf = round_weight("w2_bf", w2_raw)
         w2_codes, w2_scales = quantize("w2", w2_bf[:].rearrange("p t m j -> p (t m j)"))
-        unit_sb = tile("unit_sb", [P, PACK], F32, "w2_bf")
-        nc.sync.dma_start(unit_sb[:], unit.rearrange("(p t) o -> p (t o)", t=PACK))
         x_bytes = gather("x_bytes", xs_table, offs_sb, U8)
-        x_picked = (gather("x_codes", xw_table, offs_sb, U32, "xs_table"), x_bytes)
+        x_picked = (gather("x_codes", xw_table, offs_sb, U32), x_bytes)
         gates = []
         for t in range(PACK):
             bank = ps.tile([P, S], F32, name="gate_bank%d" % t, tag="bank%d" % t)
             product(bank, (w2_codes[:, t * P : (t + 1) * P], w2_scales[:, t * P : (t + 1) * P]), x_picked)
             gates.append(bank)
+        e_bytes = gather("e_bytes", es_table, qry_sb, U8)
 
-        def gate(t):
-            th = tile("th%d" % t, [P, 2, V], F32)
-            nc.scalar.activation(th[:], gates[t][:].rearrange("p (v d) -> p d v", d=2), ACT.Tanh, scale=0.5)
+        def gate(th, t):
+            nc.scalar.activation(th, gates[t][:].rearrange("p (v d) -> p d v", d=2), ACT.Tanh, scale=0.5)
             return th
 
-        ths = [gate(t) for t in range(PACK)]
-        w1_bf = tile("w1_bf", [P, PACK, P, PACK], BF16, "xw_table")
-        w1_source = w1_raw[:].rearrange("p j (m t) -> p m j t", t=PACK)
-        for t in range(0, PACK, 2):
-            nc.vector.tensor_copy(w1_bf[:, t : t + 2].rearrange("p t m j -> p m j t"), w1_source[:, :, :, t : t + 2])
-        ndw_table = tile("ndw_table", [P, W], F32, "w1_raw")
-        nc.sync.dma_start(ndw_table[:], ndw)
+        th_first = tile("th_first", [P, 2, V], F32)
+        ths = [gate(th_first[:], 0)]
+        w1_bf = round_weight("w1_bf", w1_raw)
+        th_rest = tile("th_rest", [P, PACK - 1, 2, V], F32, "w1_raw")
+        ths.extend(gate(th_rest[:, t - 1], t) for t in range(1, PACK))
         values = []
         for t in range(PACK):
             bank = ps.tile([P, S], F32, name="value_bank%d" % t, tag="bank%d" % (PACK + t))
             product(bank, quantize("w1_%d" % t, w1_bf[:, t].rearrange("p m j -> p (m j)")), x_picked)
             values.append(bank)
 
-        e_bytes = gather("e_bytes", es_table, qry_sb, U8, "xw_table")
-        hid_planes = tile("hid_planes", [P, PACK, V], BF16)
         last = PACK - 1
-        for t in range(PACK):
-            gated = tile("gated%d" % t, [P, 2, V], F32)
+        gated, inv_rms = [], []
+
+        def apply_gate(t):
+            gated.append(tile("gated%d" % t, [P, 2, V], F32))
             nc.vector.scalar_tensor_tensor(
-                gated[:], ths[t][:], 1.0, values[t][:].rearrange("p (v d) -> p d v", d=2), ALU.add, ALU.mult
+                gated[t][:], ths[t], 1.0, values[t][:].rearrange("p (v d) -> p d v", d=2), ALU.add, ALU.mult
             )
-            nc.vector.tensor_tensor(pooled[:, t, :V], gated[:, 0, :], gated[:, 1, :], ALU.max)
+
+        def pool_pairs(t):
+            nc.vector.tensor_tensor(pooled[:, t, :V], gated[t][:, 0, :], gated[t][:, 1, :], ALU.max)
             squares = tile("squares%d" % t, [P, V + 1], BF16)
             mean_sq = tile("mean_sq%d" % t, [P, 1], F32)
             nc.scalar.activation(squares[:], pooled[:, t, : V + 1], ACT.Square, scale=1.0 / math.sqrt(V), accum_out=mean_sq[:])
-            inv_rms = tile("inv_rms%d" % t, [P, 1], F32)
-            nc.gpsimd.tensor_tensor(inv_rms[:], mean_sq[:], minus_half[:], ALU.pow)
-            if t < last:
+            inv_rms.append(tile("inv_rms%d" % t, [P, 1], F32))
+            nc.gpsimd.tensor_tensor(inv_rms[t][:], mean_sq[:], minus_half[:], ALU.pow)
+
+        apply_gate(0)
+        for t in range(1, PACK):
+            apply_gate(t)
+            pool_pairs(t - 1)
+        pool_pairs(last)
+        e_picked = (gather("e_codes", ew_table, qry_sb, U32, "gated%d" % last), e_bytes)
+        hid_planes = tile("hid_planes", [P, PACK, V], BF16, "squares%d" % last)
+        for t in range(PACK):
+            if t < SCALAR_PLANES:
                 factor = tile("factor%d" % t, [P, 1], F32)
-                nc.gpsimd.tensor_tensor(factor[:], inv_rms[:], unit_sb[:, t : t + 1], ALU.mult)
+                nc.gpsimd.tensor_tensor(factor[:], inv_rms[t][:], unit_sb[:, t : t + 1], ALU.mult)
                 nc.scalar.activation(hid_planes[:, t, :], pooled[:, t, :V], ACT.Copy, scale=factor[:])
             else:
-                e_picked = (gather("e_codes", ew_table, qry_sb, U32, "gated%d" % last), e_bytes)
                 nc.vector.tensor_scalar(
-                    hid_planes[:, t, :], pooled[:, t, :V], inv_rms[:], unit_sb[:, t : t + 1], ALU.mult, ALU.mult
+                    hid_planes[:, t, :], pooled[:, t, :V], inv_rms[t][:], unit_sb[:, t : t + 1], ALU.mult, ALU.mult
                 )
+        weight = tile("weight", [P, Z], F32, "mean_sq%d" % last)
+        nc.scalar.activation(weight[:], ndw_table[:].indirect(qry_sb[:]), ACT.Copy)
 
         hids = []
         for h in range(2):
@@ -165,45 +183,40 @@ def tile_picked_yrerank_pair_p_kernel(
                 hid_planes[:, :, h * P : (h + 1) * P].rearrange("p t (c i) -> p c t i", i=4),
             )
             hids.append(hid)
-        banks, scores = [], []
+        halves = [slice(c * HALF, (c + 1) * HALF) for c in range(2)]
+        banks, scores = {}, []
         for h in range(2):
-            bank = ps.tile([P, Z], F32, name="score_bank%d" % h, tag="bank%d" % h)
-            product(bank, quantize("hid%d" % h, hids[h][:].rearrange("p v t -> p (v t)")), e_picked)
-            score = tile("score%d" % h, [P, Z], F32)
-            nc.scalar.copy(score[:], bank[:])
-            banks.append(bank)
-            scores.append(score)
-
-        weight = gather("weight", ndw_table, qry_sb, F32, "hid1")
+            hid_q = quantize("hid%d" % h, hids[h][:].rearrange("p v t -> p (v t)"))
+            scores.append(tile("score%d" % h, [P, Z], F32))
+            for c, copy in enumerate((nc.scalar.copy, nc.vector.tensor_copy)):
+                banks[h, c] = ps.tile([P, HALF], F32, name="score_bank%d_%d" % (h, c), tag="bank%d" % (2 * h + c))
+                product(banks[h, c], hid_q, (e_picked[0][:, halves[c]], e_picked[1][:, halves[c]]))
+                copy(scores[h][:, halves[c]], banks[h, c][:])
 
         gap = tile("gap", [P, 2, Z], F32)
         squashed = tile("squashed", [P, 2, Z], F32)
         grown = tile("grown", [P, 2, Z], F32)
-        partners = {}
         for h in range(2):
+            partners = []
             for c in range(2):
                 partner = tile("partner%d_%d" % (h, c), [P, HALF], F32)
                 window = scores[h][:].indirect(prtn_sb[:, c * HALF // 16 : (c + 1) * HALF // 16])
-                if h == 0:
-                    nc.vector.tensor_copy(partner[:], window)
-                else:
+                if c == 0:
                     nc.scalar.activation(partner[:], window, ACT.Copy)
-                partners[h, c] = partner
+                else:
+                    nc.vector.tensor_copy(partner[:], window)
+                partners.append(partner)
+            for c in range(2):
+                nc.vector.tensor_tensor(gap[:, h, halves[c]], banks[h, c][:], partners[c][:], ALU.subtract)
+                nc.scalar.activation(squashed[:, h, halves[c]], gap[:, h, halves[c]], ACT.Tanh)
+            for c in range(2):
+                nc.scalar.activation(grown[:, h, halves[c]], squashed[:, h, halves[c]], ACT.Exp, scale=-1.5)
+
+        logs = tile("logs", [P, 2, Z], F32, "squashed")
         for h in range(2):
             for c in range(2):
                 cols = slice(c * HALF, (c + 1) * HALF)
-                nc.vector.tensor_tensor(gap[:, h, cols], banks[h][:, cols], partners[h, c][:], ALU.subtract)
-                nc.scalar.activation(squashed[:, h, cols], gap[:, h, cols], ACT.Tanh)
-        for h in range(2):
-            nc.scalar.activation(grown[:, h, :], squashed[:, h, :], ACT.Exp, scale=-1.5)
-
-        out_view = out.rearrange("(h p) e -> p h e", h=2)
-        for c in range(Z // OUT_COLS):
-            cols = slice(c * OUT_COLS, (c + 1) * OUT_COLS)
-            logs = tile("logs%d" % c, [P, 2, OUT_COLS], F32)
-            nc.scalar.activation(logs[:], grown[:, :, cols], ACT.Ln, bias=0.5)
-            result = tile("result%d" % c, [P, 2, OUT_COLS], F32)
-            nc.vector.tensor_tensor(
-                result[:], logs[:], weight[:, cols].unsqueeze(1).to_broadcast([P, 2, OUT_COLS]), ALU.mult
-            )
-            nc.sync.dma_start(out_view[:, :, cols], result[:])
+                nc.scalar.activation(logs[:, h, cols], grown[:, h, cols], ACT.Ln, bias=0.5)
+                result = tile("result%d_%d" % (h, c), [P, HALF], F32)
+                nc.vector.tensor_tensor(result[:], logs[:, h, cols], weight[:, cols], ALU.mult)
+                nc.sync.dma_start(out[h * P : (h + 1) * P, cols], result[:])

@@ -42,7 +42,14 @@ def tile_picked_yrerank_pair_p_kernel(
             nc.sync.dma_start(table[:].bitcast(I32), words[0].rearrange("p n t -> p (n t)").bitcast(I32))
             return table
 
-        def load_scales(name, scales):
+        def load_scales(name, scales, clear, queue):
+            table = tile(name, [P, scales.shape[2]], U8)
+            clear.memset(table[:].bitcast(I32), 0)
+            for r in range(4):
+                queue.dma_start(table[r:P:32, :].bitcast(I32), scales[0, r:16:4, :].bitcast(I32))
+            return table
+
+        def load_scales_repeated(name, scales):
             table = tile(name, [P, scales.shape[2]], U8)
             for q in range(4):
                 rows = scales[0, 4 * q : 4 * q + 4, :].bitcast(I32)
@@ -87,16 +94,11 @@ def tile_picked_yrerank_pair_p_kernel(
         offs_sb = load_list("offs_sb", offs)
         qry_sb = load_list("qry_sb", qry)
         w2_raw = load_weight("w2_raw", w2)
-        xs_table = load_scales("xs_table", x_scales)
+        xs_table = load_scales_repeated("xs_table", x_scales)
         xw_table = load_words("xw_table", x_words)
-        es_table = load_scales("es_table", e_scales)
         w1_raw = load_weight("w1_raw", w1)
-        unit_sb = tile("unit_sb", [P, PACK], F32)
-        nc.sync.dma_start(unit_sb[:], unit.rearrange("(p t) o -> p (t o)", t=PACK))
         prtn_sb = load_list("prtn_sb", prtn)
-        ew_table = load_words("ew_table", e_words)
-        ndw_table = tile("ndw_table", [P, W], F32)
-        nc.sync.dma_start(ndw_table[:], ndw)
+        es_table = load_scales("es_table", e_scales, nc.gpsimd, nc.gpsimd)
 
         pooled = tile("pooled", [P, PACK, POOL_PITCH], F32)
         ones = tile("ones", [P, PACK], F32)
@@ -105,8 +107,8 @@ def tile_picked_yrerank_pair_p_kernel(
         minus_half = tile("minus_half", [P, 1], F32)
         nc.gpsimd.memset(minus_half[:], -0.5)
 
-        def round_weight(name, raw):
-            rounded = tile(name, [P, PACK, P, PACK], BF16)
+        def round_weight(name, raw, tag=None):
+            rounded = tile(name, [P, PACK, P, PACK], BF16, tag)
             dealt = rounded[:].rearrange("p t m j -> p m j t")
             source = raw[:].rearrange("p j (m t) -> p m j t", t=PACK)
             nc.vector.tensor_copy(dealt[:, :VECTOR_COLS], source[:, :VECTOR_COLS])
@@ -114,7 +116,10 @@ def tile_picked_yrerank_pair_p_kernel(
             return rounded
 
         w2_bf = round_weight("w2_bf", w2_raw)
+        ew_table = load_words("ew_table", e_words, "w2_raw")
         w2_codes, w2_scales = quantize("w2", w2_bf[:].rearrange("p t m j -> p (t m j)"))
+        unit_sb = tile("unit_sb", [P, PACK], F32, "w2_bf")
+        nc.sync.dma_start(unit_sb[:], unit.rearrange("(p t) o -> p (t o)", t=PACK))
         x_bytes = gather("x_bytes", xs_table, offs_sb, U8)
         x_picked = (gather("x_codes", xw_table, offs_sb, U32), x_bytes)
         gates = []
@@ -122,7 +127,7 @@ def tile_picked_yrerank_pair_p_kernel(
             bank = ps.tile([P, S], F32, name="gate_bank%d" % t, tag="bank%d" % t)
             product(bank, (w2_codes[:, t * P : (t + 1) * P], w2_scales[:, t * P : (t + 1) * P]), x_picked)
             gates.append(bank)
-        e_bytes = gather("e_bytes", es_table, qry_sb, U8)
+        e_bytes = gather("e_bytes", es_table, qry_sb, U8, "xw_table")
 
         def gate(th, t):
             nc.scalar.activation(th, gates[t][:].rearrange("p (v d) -> p d v", d=2), ACT.Tanh, scale=0.5)
@@ -130,7 +135,7 @@ def tile_picked_yrerank_pair_p_kernel(
 
         th_first = tile("th_first", [P, 2, V], F32)
         ths = [gate(th_first[:], 0)]
-        w1_bf = round_weight("w1_bf", w1_raw)
+        w1_bf = round_weight("w1_bf", w1_raw, "es_table")
         th_rest = tile("th_rest", [P, PACK - 1, 2, V], F32, "w1_raw")
         ths.extend(gate(th_rest[:, t - 1], t) for t in range(1, PACK))
         values = []
@@ -138,6 +143,9 @@ def tile_picked_yrerank_pair_p_kernel(
             bank = ps.tile([P, S], F32, name="value_bank%d" % t, tag="bank%d" % (PACK + t))
             product(bank, quantize("w1_%d" % t, w1_bf[:, t].rearrange("p m j -> p (m j)")), x_picked)
             values.append(bank)
+
+        ndw_table = tile("ndw_table", [P, W], F32, "es_table")
+        nc.sync.dma_start(ndw_table[:], ndw)
 
         last = PACK - 1
         gated, inv_rms = [], []

import math
from contextlib import ExitStack

import concourse.mybir as mybir

K, T, S, H, Z, W = 512, 2048, 512, 512, 512, 2048
V = S // 2
P = 128
PACK = 4
FLOPS = 2 * K * H * S * 2 + 2 * H * V * Z

F32 = mybir.dt.float32
BF16 = mybir.dt.bfloat16
U32 = mybir.dt.uint32
I32 = mybir.dt.int32
U16 = mybir.dt.uint16
U8 = mybir.dt.uint8
FP8X4 = mybir.dt.float8_e4m3fn_x4
ALU = mybir.AluOpType
ACT = mybir.ActivationFunctionType

EPS = 0.1
VECTOR_COLS = 88
POOL_PITCH = V + 8
SCALAR_PLANES = 2
HALF = Z // 2


def tile_picked_yrerank_pair_p_kernel(
    tc, x_words, x_scales, w1, w2, e_words, e_scales, unit, ndw, offs, qry, prtn, out
):
    nc = tc.nc
    with ExitStack() as ctx:
        sb = ctx.enter_context(tc.tile_pool(name="sb", bufs=1))
        ps = ctx.enter_context(tc.psum_pool(name="ps", bufs=1))

        def tile(name, shape, dtype, tag=None):
            return sb.tile(shape, dtype, name=name, tag=tag or name, align_bytes=64)

        def load_words(name, words, tag=None):
            table = tile(name, [P, words.shape[2]], U32, tag)
            nc.sync.dma_start(table[:].bitcast(I32), words[0].rearrange("p n t -> p (n t)").bitcast(I32))
            return table

        def load_scales(name, scales, clear, queue):
            table = tile(name, [P, scales.shape[2]], U8)
            clear.memset(table[:].bitcast(I32), 0)
            for r in range(4):
                queue.dma_start(table[r:P:32, :].bitcast(I32), scales[0, r:16:4, :].bitcast(I32))
            return table

        def load_scales_repeated(name, scales):
            table = tile(name, [P, scales.shape[2]], U8)
            for q in range(4):
                rows = scales[0, 4 * q : 4 * q + 4, :].bitcast(I32)
                nc.sync.dma_start(
                    table[32 * q : 32 * q + 32, :].bitcast(I32), rows.unsqueeze(0).to_broadcast([8] + list(rows.shape))
                )
            return table

        def load_list(name, entries):
            offsets = tile(name, [P, entries.shape[1]], U16)
            nc.sync.dma_start(offsets[:], entries)
            return offsets

        def load_weight(name, w):
            raw = tile(name, [P, PACK, H], F32)
            nc.sync.dma_start(raw[:], w.rearrange("(p j) c -> p j c", j=PACK))
            return raw

        def gather(name, table, offsets, dtype, tag=None):
            picked = tile(name, [P, 16 * offsets.shape[1]], dtype, tag)
            nc.vector.tensor_copy(picked[:], table[:].indirect(offsets[:]))
            return picked[:]

        def quantize(name, values):
            width = values.shape[1] // PACK
            codes = tile(name + "_codes", [P, width], U32)
            scales = tile(name + "_scales", [P, width], U8)
            nc.vector.quantize_mx(out=codes[:].bitcast(FP8X4), scales=scales[:], in_=values)
            return codes[:], scales[:]

        def product(bank, stationary, moving):
            nc.tensor.matmul_mx(
                out=bank[:],
                lhsT=stationary[0].bitcast(FP8X4),
                lhsT_scale=stationary[1],
                rhs=moving[0].bitcast(FP8X4),
                rhs_scale=moving[1],
                start=True,
                stop=True,
            )

        offs_sb = load_list("offs_sb", offs)
        qry_sb = load_list("qry_sb", qry)
        w2_raw = load_weight("w2_raw", w2)
        xs_table = load_scales_repeated("xs_table", x_scales)
        xw_table = load_words("xw_table", x_words)
        w1_raw = load_weight("w1_raw", w1)
        prtn_sb = load_list("prtn_sb", prtn)
        es_table = load_scales("es_table", e_scales, nc.gpsimd, nc.gpsimd)

        pooled = tile("pooled", [P, PACK, POOL_PITCH], F32)
        ones = tile("ones", [P, PACK], F32)
        nc.gpsimd.memset(ones[:], 1.0)
        nc.gpsimd.tensor_scalar(pooled[:, :, V], ones[:], math.sqrt(4.0 * EPS * V), 0.0, ALU.mult, ALU.add)
        minus_half = tile("minus_half", [P, 1], F32)
        nc.gpsimd.memset(minus_half[:], -0.5)

        def round_weight(name, raw, tag=None):
            rounded = tile(name, [P, PACK, P, PACK], BF16, tag)
            dealt = rounded[:].rearrange("p t m j -> p m j t")
            source = raw[:].rearrange("p j (m t) -> p m j t", t=PACK)
            nc.vector.tensor_copy(dealt[:, :VECTOR_COLS], source[:, :VECTOR_COLS])
            nc.scalar.copy(dealt[:, VECTOR_COLS:], source[:, VECTOR_COLS:])
            return rounded

        w2_bf = round_weight("w2_bf", w2_raw)
        ew_table = load_words("ew_table", e_words, "w2_raw")
        w2_codes, w2_scales = quantize("w2", w2_bf[:].rearrange("p t m j -> p (t m j)"))
        unit_sb = tile("unit_sb", [P, PACK], F32, "w2_bf")
        nc.sync.dma_start(unit_sb[:], unit.rearrange("(p t) o -> p (t o)", t=PACK))
        x_bytes = gather("x_bytes", xs_table, offs_sb, U8)
        x_picked = (gather("x_codes", xw_table, offs_sb, U32), x_bytes)
        gates = []
        for t in range(PACK):
            bank = ps.tile([P, S], F32, name="gate_bank%d" % t, tag="bank%d" % t)
            product(bank, (w2_codes[:, t * P : (t + 1) * P], w2_scales[:, t * P : (t + 1) * P]), x_picked)
            gates.append(bank)
        e_bytes = gather("e_bytes", es_table, qry_sb, U8, "xw_table")

        def gate(th, t):
            nc.scalar.activation(th, gates[t][:].rearrange("p (v d) -> p d v", d=2), ACT.Tanh, scale=0.5)
            return th

        th_first = tile("th_first", [P, 2, V], F32)
        ths = [gate(th_first[:], 0)]
        w1_bf = round_weight("w1_bf", w1_raw, "es_table")
        th_rest = tile("th_rest", [P, PACK - 1, 2, V], F32, "w1_raw")
        ths.extend(gate(th_rest[:, t - 1], t) for t in range(1, PACK))
        values = []
        for t in range(PACK):
            bank = ps.tile([P, S], F32, name="value_bank%d" % t, tag="bank%d" % (PACK + t))
            product(bank, quantize("w1_%d" % t, w1_bf[:, t].rearrange("p m j -> p (m j)")), x_picked)
            values.append(bank)

        ndw_table = tile("ndw_table", [P, W], F32, "es_table")
        nc.sync.dma_start(ndw_table[:], ndw)

        last = PACK - 1
        gated, inv_rms = [], []

        def apply_gate(t):
            gated.append(tile("gated%d" % t, [P, 2, V], F32))
            nc.vector.scalar_tensor_tensor(
                gated[t][:], ths[t], 1.0, values[t][:].rearrange("p (v d) -> p d v", d=2), ALU.add, ALU.mult
            )

        def pool_pairs(t):
            nc.vector.tensor_tensor(pooled[:, t, :V], gated[t][:, 0, :], gated[t][:, 1, :], ALU.max)
            squares = tile("squares%d" % t, [P, V + 1], BF16)
            mean_sq = tile("mean_sq%d" % t, [P, 1], F32)
            nc.scalar.activation(squares[:], pooled[:, t, : V + 1], ACT.Square, scale=1.0 / math.sqrt(V), accum_out=mean_sq[:])
            inv_rms.append(tile("inv_rms%d" % t, [P, 1], F32))
            nc.gpsimd.tensor_tensor(inv_rms[t][:], mean_sq[:], minus_half[:], ALU.pow)

        apply_gate(0)
        for t in range(1, PACK):
            apply_gate(t)
            pool_pairs(t - 1)
        pool_pairs(last)
        e_picked = (gather("e_codes", ew_table, qry_sb, U32, "gated%d" % last), e_bytes)
        hid_planes = tile("hid_planes", [P, PACK, V], BF16, "squares%d" % last)
        for t in range(PACK):
            if t < SCALAR_PLANES:
                factor = tile("factor%d" % t, [P, 1], F32)
                nc.gpsimd.tensor_tensor(factor[:], inv_rms[t][:], unit_sb[:, t : t + 1], ALU.mult)
                nc.scalar.activation(hid_planes[:, t, :], pooled[:, t, :V], ACT.Copy, scale=factor[:])
            else:
                nc.vector.tensor_scalar(
                    hid_planes[:, t, :], pooled[:, t, :V], inv_rms[t][:], unit_sb[:, t : t + 1], ALU.mult, ALU.mult
                )
        weight = tile("weight", [P, Z], F32, "mean_sq%d" % last)
        nc.scalar.activation(weight[:], ndw_table[:].indirect(qry_sb[:]), ACT.Copy)

        hids = []
        for h in range(2):
            hid = tile("hid%d" % h, [P, P, PACK], BF16)
            nc.vector.tensor_copy(
                hid[:].rearrange("p (c i) t -> p c t i", i=4),
                hid_planes[:, :, h * P : (h + 1) * P].rearrange("p t (c i) -> p c t i", i=4),
            )
            hids.append(hid)
        halves = [slice(c * HALF, (c + 1) * HALF) for c in range(2)]
        banks, scores = {}, []
        for h in range(2):
            hid_q = quantize("hid%d" % h, hids[h][:].rearrange("p v t -> p (v t)"))
            scores.append(tile("score%d" % h, [P, Z], F32))
            for c, copy in enumerate((nc.scalar.copy, nc.vector.tensor_copy)):
                banks[h, c] = ps.tile([P, HALF], F32, name="score_bank%d_%d" % (h, c), tag="bank%d" % (2 * h + c))
                product(banks[h, c], hid_q, (e_picked[0][:, halves[c]], e_picked[1][:, halves[c]]))
                copy(scores[h][:, halves[c]], banks[h, c][:])

        gap = tile("gap", [P, 2, Z], F32)
        squashed = tile("squashed", [P, 2, Z], F32)
        grown = tile("grown", [P, 2, Z], F32)
        for h in range(2):
            partners = []
            for c in range(2):
                partner = tile("partner%d_%d" % (h, c), [P, HALF], F32)
                window = scores[h][:].indirect(prtn_sb[:, c * HALF // 16 : (c + 1) * HALF // 16])
                if c == 0:
                    nc.scalar.activation(partner[:], window, ACT.Copy)
                else:
                    nc.vector.tensor_copy(partner[:], window)
                partners.append(partner)
            for c in range(2):
                nc.vector.tensor_tensor(gap[:, h, halves[c]], banks[h, c][:], partners[c][:], ALU.subtract)
                nc.scalar.activation(squashed[:, h, halves[c]], gap[:, h, halves[c]], ACT.Tanh)
            for c in range(2):
                nc.scalar.activation(grown[:, h, halves[c]], squashed[:, h, halves[c]], ACT.Exp, scale=-1.5)

        logs = tile("logs", [P, 2, Z], F32, "squashed")
        for h in range(2):
            for c in range(2):
                cols = slice(c * HALF, (c + 1) * HALF)
                nc.scalar.activation(logs[:, h, cols], grown[:, h, cols], ACT.Ln, bias=0.5)
                result = tile("result%d_%d" % (h, c), [P, HALF], F32)
                nc.vector.tensor_tensor(result[:], logs[:, h, cols], weight[:, cols], ALU.mult)
                nc.sync.dma_start(out[h * P : (h + 1) * P, cols], result[:])
